import numpy as np
import ml_dtypes

BF16 = ml_dtypes.bfloat16


def bf(x):
    return np.asarray(x, np.float32).astype(BF16)


def f32(x):
    return np.asarray(x, np.float32)


def f64(x):
    return np.asarray(x).astype(np.float64)


def striped(idx):
    return np.tile(idx.reshape(-1, 16).T, (8, 1))


S, K, M, N, E, Q = 256, 128, 256, 256, 4, 64


def setup_inputs():
    return {"base": bf(np.random.standard_normal((M, S))), "x": bf(np.random.standard_normal((K, N))), "w": bf(np.random.standard_normal((E, K, M)) / np.sqrt(K)), "offs": striped(np.random.permutation(S))}


def reference(base, x, w, offs):
    idx = offs[:16].T.reshape(-1)
    z = f64(base).copy()
    for e in range(E):
        z[:, idx[e * Q : (e + 1) * Q]] += f64(w)[e].T @ f64(x)[:, e * Q : (e + 1) * Q]
    return z

@@ -1,0 +1,56 @@
+import concourse.mybir as mybir
+from concourse.masks import make_identity
+
+BF16, F32, U16 = mybir.dt.bfloat16, mybir.dt.float32, mybir.dt.uint16
+
+P = 128
+TOKENS = 256
+ROWS = 256
+K = 128
+N = 256
+EXPERTS = 4
+PIECE = N // EXPERTS
+PER_COLUMN = 16
+BLOCKS = ROWS // P
+
+FLOPS = 2 * ROWS * K * N
+
+
+def tile_scatter_matmul_kernel(tc, base, x, w, offs, out):
+    nc = tc.nc
+    with (
+        tc.tile_pool(name="held", bufs=1) as held,
+        tc.psum_pool(name="psum", bufs=1) as psum,
+    ):
+        base_tile = held.tile([P, BLOCKS, TOKENS], BF16, name="base_tile")
+        w_tile = held.tile([P, EXPERTS, ROWS], BF16, name="w_tile")
+        x_tile = held.tile([P, N], BF16, name="x_tile")
+        offsets = held.tile([P, N // PER_COLUMN], U16, name="offsets")
+        nc.sync.dma_start(base_tile[:], base.rearrange("(b p) s -> p b s", p=P))
+        nc.sync.dma_start(w_tile[:], w.rearrange("e k m -> k e m"))
+        nc.sync.dma_start(x_tile[:], x)
+        nc.sync.dma_start(offsets[:], offs)
+
+        ident = held.tile([P, P], BF16, name="ident")
+        make_identity(nc, ident[:])
+
+        windows = [psum.tile([P, TOKENS], F32, name=f"window{b}") for b in range(BLOCKS)]
+        for b in range(BLOCKS):
+            nc.tensor.matmul(windows[b][:], ident[:], base_tile[:, b, :], start=True, stop=False)
+
+        for b in range(BLOCKS):
+            for e in range(EXPERTS):
+                entries = slice(e * PIECE, (e + 1) * PIECE)
+                columns = slice(e * PIECE // PER_COLUMN, (e + 1) * PIECE // PER_COLUMN)
+                nc.tensor.matmul(
+                    windows[b][:].indirect(offsets[:, columns]),
+                    w_tile[:, e, b * P : (b + 1) * P],
+                    x_tile[:, entries],
+                    start=False,
+                    stop=(e == EXPERTS - 1),
+                )
+
+        for b in range(BLOCKS):
+            z = held.tile([P, TOKENS], F32, name=f"z{b}")
+            nc.vector.tensor_copy(z[:], windows[b][:])
+            nc.sync.dma_start(out[b * P : (b + 1) * P, :], z[:])

@@ -12,6 +12,8 @@ EXPERTS = 4
 PIECE = N // EXPERTS
 PER_COLUMN = 16
 BLOCKS = ROWS // P
+BANK = 512
+WARM_UPS = 4
 
 FLOPS = 2 * ROWS * K * N
 
@@ -30,6 +32,12 @@ def tile_scatter_matmul_kernel(tc, base, x, w, offs, out):
         nc.sync.dma_start(w_tile[:], w.rearrange("e k m -> k e m"))
         nc.sync.dma_start(x_tile[:], x)
         nc.sync.dma_start(offsets[:], offs)
+
+        zeros = held.tile([P, BANK], BF16, name="zeros")
+        nc.vector.memset(zeros[:], 0.0)
+        spare = psum.tile([P, BANK], F32, name="spare")
+        for _ in range(WARM_UPS):
+            nc.tensor.matmul(spare[:], zeros[:, :P], zeros[:], start=True, stop=True)
 
         ident = held.tile([P, P], BF16, name="ident")
         make_identity(nc, ident[:])

@@ -12,8 +12,7 @@ EXPERTS = 4
 PIECE = N // EXPERTS
 PER_COLUMN = 16
 BLOCKS = ROWS // P
-BANK = 512
-WARM_UPS = 4
+WARM_UPS = 6
 
 FLOPS = 2 * ROWS * K * N
 
@@ -33,9 +32,9 @@ def tile_scatter_matmul_kernel(tc, base, x, w, offs, out):
         nc.sync.dma_start(x_tile[:], x)
         nc.sync.dma_start(offsets[:], offs)
 
-        zeros = held.tile([P, BANK], BF16, name="zeros")
-        nc.vector.memset(zeros[:], 0.0)
-        spare = psum.tile([P, BANK], F32, name="spare")
+        zeros = held.tile([P, TOKENS], BF16, name="zeros")
+        nc.gpsimd.memset(zeros[:], 0.0)
+        spare = psum.tile([P, TOKENS], F32, name="spare")
         for _ in range(WARM_UPS):
             nc.tensor.matmul(spare[:], zeros[:, :P], zeros[:], start=True, stop=True)
 

import concourse.mybir as mybir
from concourse.masks import make_identity

BF16, F32, U16 = mybir.dt.bfloat16, mybir.dt.float32, mybir.dt.uint16

P = 128
TOKENS = 256
ROWS = 256
K = 128
N = 256
EXPERTS = 4
PIECE = N // EXPERTS
PER_COLUMN = 16
BLOCKS = ROWS // P
WARM_UPS = 6

FLOPS = 2 * ROWS * K * N


def tile_scatter_matmul_kernel(tc, base, x, w, offs, out):
    nc = tc.nc
    with (
        tc.tile_pool(name="held", bufs=1) as held,
        tc.psum_pool(name="psum", bufs=1) as psum,
    ):
        base_tile = held.tile([P, BLOCKS, TOKENS], BF16, name="base_tile")
        w_tile = held.tile([P, EXPERTS, ROWS], BF16, name="w_tile")
        x_tile = held.tile([P, N], BF16, name="x_tile")
        offsets = held.tile([P, N // PER_COLUMN], U16, name="offsets")
        nc.sync.dma_start(base_tile[:], base.rearrange("(b p) s -> p b s", p=P))
        nc.sync.dma_start(w_tile[:], w.rearrange("e k m -> k e m"))
        nc.sync.dma_start(x_tile[:], x)
        nc.sync.dma_start(offsets[:], offs)

        zeros = held.tile([P, TOKENS], BF16, name="zeros")
        nc.gpsimd.memset(zeros[:], 0.0)
        spare = psum.tile([P, TOKENS], F32, name="spare")
        for _ in range(WARM_UPS):
            nc.tensor.matmul(spare[:], zeros[:, :P], zeros[:], start=True, stop=True)

        ident = held.tile([P, P], BF16, name="ident")
        make_identity(nc, ident[:])

        windows = [psum.tile([P, TOKENS], F32, name=f"window{b}") for b in range(BLOCKS)]
        for b in range(BLOCKS):
            nc.tensor.matmul(windows[b][:], ident[:], base_tile[:, b, :], start=True, stop=False)

        for b in range(BLOCKS):
            for e in range(EXPERTS):
                entries = slice(e * PIECE, (e + 1) * PIECE)
                columns = slice(e * PIECE // PER_COLUMN, (e + 1) * PIECE // PER_COLUMN)
                nc.tensor.matmul(
                    windows[b][:].indirect(offsets[:, columns]),
                    w_tile[:, e, b * P : (b + 1) * P],
                    x_tile[:, entries],
                    start=False,
                    stop=(e == EXPERTS - 1),
                )

        for b in range(BLOCKS):
            z = held.tile([P, TOKENS], F32, name=f"z{b}")
            nc.vector.tensor_copy(z[:], windows[b][:])
            nc.sync.dma_start(out[b * P : (b + 1) * P, :], z[:])
